import numpy as np
import ml_dtypes


def mxq(x, axis, fmt="e4m3"):
    dtype, down = {"e4m3": (ml_dtypes.float8_e4m3fn, 7), "e5m2": (ml_dtypes.float8_e5m2, 14)}[fmt]
    v = np.moveaxis(np.asarray(x, np.float32).astype(ml_dtypes.bfloat16).astype(np.float64), axis, -1)
    blocks = v.reshape(v.shape[:-1] + (-1, 32))
    amax = np.abs(blocks).max(-1, keepdims=True)
    byte = np.maximum(np.where(amax > 0, np.frexp(amax)[1] - 1 + 127, 0) - down, 1)
    scale = np.exp2(byte - 127.0)
    codes = (blocks / scale).astype(np.float32).astype(dtype).astype(np.float64)
    return np.moveaxis((codes * scale).reshape(v.shape), -1, axis)


WIDE = False


def mx_kscale(k):
    if not WIDE:
        return np.ones(k)
    levels = np.array([10, -10, 5, -5, 0])
    if k % 512:
        return np.exp2(np.random.permutation(np.resize(levels, k // 32))).repeat(32)
    a = np.empty((k // 512, 16))
    for p in range(k // 512):
        a[p, :8] = np.random.permutation(np.resize(levels, 8))
        for g in range(8):
            far = levels[np.abs(levels - a[p, g]) >= 10]
            a[p, g + 8] = far[np.random.randint(len(far))]
    return np.exp2(a.ravel()).repeat(32)


def f64(x):
    return np.asarray(x).astype(np.float64)


def striped(idx):
    return np.tile(idx.reshape(-1, 16).T, (8, 1)).astype(np.uint16)


def unstriped(offs):
    return offs[:16].T.reshape(-1).astype(np.int64)


def relu2(v):
    return np.maximum(v, 0.0) ** 2


K, T, E, C, N = 1536, 1536, 6, 256, 128


def by_expert(wq, xq):
    return np.concatenate([wq[e].T @ xq[:, e * C:(e + 1) * C] for e in range(E)], axis=1)


def setup_inputs():
    n = np.random.standard_normal
    s = mx_kscale(K)[:, None]
    return {
        "xT": (n((K, T)) * s).astype(np.float32),
        "w": (n((E, K, N)) / np.sqrt(K) / s[None]).astype(np.float32),
        "b": (0.3 * n((N, E))).astype(np.float32),
        "gate": np.tile(np.random.uniform(0.2, 1.0, E * C), (N, 1)).astype(np.float32),
        "offs": striped(np.random.permutation(T)[:E * C]),
        "dst": striped(np.random.permutation(T)[:E * C]),
    }


def reference(xT, w, b, gate, offs, dst):
    idx = unstriped(offs)
    xq = mxq(f64(xT)[:, idx], 0, "e4m3")
    y = by_expert(mxq(f64(w), 1, "e4m3"), xq)
    y = relu2(y + np.repeat(f64(b), C, axis=1))
    out = np.zeros((N, T))
    out[:, unstriped(dst)] = f64(gate) * y
    return out

@@ -1,0 +1,191 @@
+from contextlib import ExitStack
+
+import concourse.mybir as mybir
+
+K, T, E, C, N = 1536, 1536, 6, 256, 128
+FLOPS = 2 * E * C * K * N
+
+F32 = mybir.dt.float32
+BF16 = mybir.dt.bfloat16
+U32 = mybir.dt.uint32
+I32 = mybir.dt.int32
+U16 = mybir.dt.uint16
+U8 = mybir.dt.uint8
+FP8X4 = mybir.dt.float8_e4m3fn_x4
+ACT = mybir.ActivationFunctionType
+MULT = mybir.AluOpType.mult
+
+P = 128
+PACK = 4
+PASSES = K // (P * PACK)
+QUAD = 4
+HALF = T // 2
+WINDOW = 2048
+
+CHUNKS = (
+    ((0, 1024, 1024, (512, 1024)), (1024, 512, 0, (512,))),
+    ((0, 512, 512, (512,)), (512, 512, 512, (512,)), (1024, 512, 256, (512,))),
+    ((0, 512, 512, (512,)), (512, 512, 320, (512,)), (1024, 256, 128, (256,)), (1280, 256, 96, (256,))),
+)
+GPSIMD_EXPERTS = (1, 3)
+ADD = mybir.AluOpType.add
+
+
+def tile_moe_two_lin_relu2_kernel(tc, xT, w, b, gate, offs, dst, out):
+    nc = tc.nc
+    with ExitStack() as ctx:
+        held = ctx.enter_context(tc.tile_pool(name="held", bufs=1))
+        xraw = ctx.enter_context(tc.tile_pool(name="xraw", bufs=1))
+        xgrp = ctx.enter_context(tc.tile_pool(name="xgrp", bufs=3))
+        wraw = ctx.enter_context(tc.tile_pool(name="wraw", bufs=1))
+        psum = ctx.enter_context(tc.psum_pool(name="psum", bufs=1))
+
+        offs_sb = held.tile([P, T // 16], U16, name="offs_sb")
+        dst_sb = held.tile([P, T // 16], U16, name="dst_sb")
+        bias = held.tile([P, E], F32, name="bias")
+        gate_sb = held.tile([P, T], F32, name="gate_sb", align_bytes=64)
+        out_sb = held.tile([P, T], F32, name="out_sb", align_bytes=64)
+        planes = held.tile([P, T], U8, name="planes", align_bytes=64)
+        g_planes = held.tile([P, T], U8, name="g_planes", align_bytes=64)
+        codes = [
+            held.tile([P, T if a == PASSES - 1 else WINDOW], U32, name=f"codes{a}", align_bytes=64)
+            for a in range(PASSES)
+        ]
+        g_codes = [held.tile([P, T], U32, name=f"g_codes{a}", align_bytes=64) for a in range(PASSES)]
+        w_codes = held.tile([P, E, PASSES, N], U32, name="w_codes", align_bytes=64)
+        w_planes = held.tile([P, E, PASSES, N], U8, name="w_planes", align_bytes=64)
+        w_grp = held.tile([P, E, PASSES, N, PACK], BF16, name="w_grp", align_bytes=64)
+        warm = held.tile([P, 1], F32, name="warm")
+
+        nc.gpsimd.memset(planes[:].bitcast(I32), 0)
+        for a in range(PASSES - 1):
+            nc.gpsimd.memset(codes[a][:, T:].bitcast(I32), 0)
+        nc.gpsimd.memset(warm[:], 0.0)
+        nc.scalar.activation(warm[:], warm[:], ACT.Relu)
+
+        raw = {}
+        for a in range(PASSES):
+            rows = xT[a * 512 : (a + 1) * 512, :].rearrange("(p j) t -> p j t", j=PACK)
+            for c0, cw, ns, ends in CHUNKS[a]:
+                lo = 0
+                for hi in ends:
+                    t = xraw.tile([P, PACK, hi - lo], F32, name=f"x{a}_{c0 + lo}")
+                    nc.sync.dma_start(out=t[:], in_=rows[:, :, c0 + lo : c0 + hi])
+                    raw[a, c0 + lo] = t
+                    lo = hi
+            if a == 0:
+                nc.sync.dma_start(offs_sb[:], offs)
+        w_raw = []
+        for e in range(E):
+            t = wraw.tile([P, PASSES, PACK * N], F32, name=f"w{e}")
+            nc.sync.dma_start(out=t[:], in_=w[e].rearrange("(a p j) n -> p a (j n)", p=P, j=PACK))
+            w_raw.append(t)
+            if e == 0:
+                nc.sync.dma_start(out=bias[:], in_=b)
+                nc.sync.dma_start(dst_sb[:], dst)
+            if e == 1:
+                nc.sync.dma_start(out=gate_sb[:], in_=gate)
+
+        def gather_words(a, h):
+            s = slice(h * HALF, (h + 1) * HALF)
+            nc.vector.tensor_copy(g_codes[a][:, s], codes[a][:].indirect(offs_sb[:, h * 48 : h * 48 + 48]))
+
+        def gather_bytes(h):
+            s = slice(h * HALF, (h + 1) * HALF)
+            nc.vector.tensor_copy(g_planes[:, s], planes[:].indirect(offs_sb[:, h * 48 : h * 48 + 48]))
+
+        for a in range(PASSES):
+            for c0, cw, ns, ends in CHUNKS[a]:
+                grp = xgrp.tile([P, cw, PACK], BF16, name=f"grp{cw}", bufs=1 if cw > 512 else 3, align_bytes=64)
+                to = grp[:].rearrange("p (c i) t -> p c t i", i=4)
+                lo = 0
+                for hi in ends:
+                    fr = raw[a, c0 + lo][:].rearrange("p t (c i) -> p c t i", i=4)
+                    mid = min(max(ns, lo), hi)
+                    if mid > lo:
+                        nc.scalar.activation(to[:, lo // 4 : mid // 4], fr[:, : (mid - lo) // 4], ACT.Copy)
+                    if hi > mid:
+                        nc.vector.tensor_copy(to[:, mid // 4 : hi // 4], fr[:, (mid - lo) // 4 :])
+                    lo = hi
+                flat = grp[:].rearrange("p w t -> p (w t)")
+                nc.vector.quantize_mx(
+                    out=codes[a][:, c0 : c0 + cw].bitcast(FP8X4),
+                    scales=planes[QUAD * a : P, c0 : c0 + cw],
+                    in_=flat,
+                )
+            if a < PASSES - 1:
+                nc.vector.tensor_copy(g_codes[a][:], codes[a][:].indirect(offs_sb[:]))
+
+        flat_codes = w_codes[:].rearrange("p e a n -> p (e a n)")
+        flat_planes = w_planes[:].rearrange("p e a n -> p (e a n)")
+        flat_grp = w_grp[:].rearrange("p e a n t -> p (e a n t)")
+
+        def w_copy(e):
+            for a in range(PASSES):
+                to = w_grp[:, e, a].rearrange("p (c i) t -> p c t i", i=4)
+                fr = w_raw[e][:, a].rearrange("p (t c i) -> p c t i", t=PACK, i=4)
+                if e in GPSIMD_EXPERTS:
+                    nc.gpsimd.tensor_scalar(to, fr, 1.0, 0.0, MULT, ADD)
+                else:
+                    nc.scalar.activation(to, fr, ACT.Copy)
+
+        def w_quant(e):
+            base = e * PASSES * N
+            for lo, hi in ((0, 512), (512, 768)):
+                nc.vector.quantize_mx(
+                    out=flat_codes[:, base + lo : base + hi].bitcast(FP8X4),
+                    scales=flat_planes[:, base + lo : base + hi],
+                    in_=flat_grp[:, PACK * (base + lo) : PACK * (base + hi)],
+                )
+
+        relu = [held.tile([P, 2 * C], F32, name=f"relu{g}") for g in range(E // 2)]
+
+        def multiply(e):
+            acc = psum.tile([P, C], F32, name=f"acc{e}")
+            cols = slice(e * C, (e + 1) * C)
+            for a in range(PASSES):
+                nc.tensor.matmul_mx(
+                    out=acc[:],
+                    lhsT=w_codes[:, e, a, :].bitcast(FP8X4),
+                    lhsT_scale=w_planes[:, e, a, :],
+                    rhs=g_codes[a][:, cols].bitcast(FP8X4),
+                    rhs_scale=g_planes[QUAD * a : P, cols],
+                    start=(a == 0),
+                    stop=(a == PASSES - 1),
+                )
+            half = e % 2 * C
+            nc.scalar.activation(relu[e // 2][:, half : half + C], acc[:], ACT.Relu, bias=bias[:, e : e + 1])
+
+        def square(g):
+            nc.scalar.activation(relu[g][:], relu[g][:], ACT.Square)
+
+        def scatter(g):
+            cols = slice(g * 2 * C, (g + 1) * 2 * C)
+            nc.vector.tensor_tensor(
+                out_sb[:].indirect(dst_sb[:, g * 32 : (g + 1) * 32]), relu[g][:], gate_sb[:, cols], MULT
+            )
+
+        for e in range(E):
+            w_copy(e)
+            if e == 1:
+                gather_words(2, 0)
+                gather_bytes(0)
+                w_quant(0)
+                gather_words(2, 1)
+                gather_bytes(1)
+            if e == 3:
+                w_quant(2)
+                multiply(0)
+                multiply(1)
+                square(0)
+                scatter(0)
+        w_quant(4)
+        multiply(2)
+        multiply(3)
+        square(1)
+        scatter(1)
+        multiply(4)
+        multiply(5)
+        square(2)
+        scatter(2)
+        nc.sync.dma_start(out=out, in_=out_sb[:])

@@ -23,11 +23,11 @@ HALF = T // 2
 WINDOW = 2048
 
 CHUNKS = (
-    ((0, 1024, 1024, (512, 1024)), (1024, 512, 0, (512,))),
-    ((0, 512, 512, (512,)), (512, 512, 512, (512,)), (1024, 512, 256, (512,))),
-    ((0, 512, 512, (512,)), (512, 512, 320, (512,)), (1024, 256, 128, (256,)), (1280, 256, 96, (256,))),
+    ((0, 512, 288), (512, 512, 512), (1024, 512, 512)),
+    ((0, 512, 512), (512, 512, 512), (1024, 512, 384)),
+    ((0, 512, 512), (512, 512, 448), (1024, 256, 160), (1280, 256, 96)),
 )
-GPSIMD_EXPERTS = (1, 3)
+GPSIMD_PASS = 2
 ADD = mybir.AluOpType.add
 
 
@@ -46,15 +46,15 @@ def tile_moe_two_lin_relu2_kernel(tc, xT, w, b, gate, offs, dst, out):
         gate_sb = held.tile([P, T], F32, name="gate_sb", align_bytes=64)
         out_sb = held.tile([P, T], F32, name="out_sb", align_bytes=64)
         planes = held.tile([P, T], U8, name="planes", align_bytes=64)
-        g_planes = held.tile([P, T], U8, name="g_planes", align_bytes=64)
         codes = [
             held.tile([P, T if a == PASSES - 1 else WINDOW], U32, name=f"codes{a}", align_bytes=64)
             for a in range(PASSES)
         ]
-        g_codes = [held.tile([P, T], U32, name=f"g_codes{a}", align_bytes=64) for a in range(PASSES)]
+        g_codes = [held.tile([P, T], U32, name=f"g_codes{a}", align_bytes=64) for a in range(PASSES - 1)]
+        last_codes = []
+        g_planes = []
         w_codes = held.tile([P, E, PASSES, N], U32, name="w_codes", align_bytes=64)
         w_planes = held.tile([P, E, PASSES, N], U8, name="w_planes", align_bytes=64)
-        w_grp = held.tile([P, E, PASSES, N, PACK], BF16, name="w_grp", align_bytes=64)
         warm = held.tile([P, 1], F32, name="warm")
 
         nc.gpsimd.memset(planes[:].bitcast(I32), 0)
@@ -66,13 +66,10 @@ def tile_moe_two_lin_relu2_kernel(tc, xT, w, b, gate, offs, dst, out):
         raw = {}
         for a in range(PASSES):
             rows = xT[a * 512 : (a + 1) * 512, :].rearrange("(p j) t -> p j t", j=PACK)
-            for c0, cw, ns, ends in CHUNKS[a]:
-                lo = 0
-                for hi in ends:
-                    t = xraw.tile([P, PACK, hi - lo], F32, name=f"x{a}_{c0 + lo}")
-                    nc.sync.dma_start(out=t[:], in_=rows[:, :, c0 + lo : c0 + hi])
-                    raw[a, c0 + lo] = t
-                    lo = hi
+            for c0, cw, ns in CHUNKS[a]:
+                t = xraw.tile([P, PACK, cw], F32, name=f"x{a}_{c0}")
+                nc.sync.dma_start(out=t[:], in_=rows[:, :, c0 : c0 + cw])
+                raw[a, c0] = t
             if a == 0:
                 nc.sync.dma_start(offs_sb[:], offs)
         w_raw = []
@@ -81,75 +78,81 @@ def tile_moe_two_lin_relu2_kernel(tc, xT, w, b, gate, offs, dst, out):
             nc.sync.dma_start(out=t[:], in_=w[e].rearrange("(a p j) n -> p a (j n)", p=P, j=PACK))
             w_raw.append(t)
             if e == 0:
-                nc.sync.dma_start(out=bias[:], in_=b)
                 nc.sync.dma_start(dst_sb[:], dst)
-            if e == 1:
-                nc.sync.dma_start(out=gate_sb[:], in_=gate)
+            if e == 3:
+                nc.sync.dma_start(out=bias[:], in_=b)
+                nc.sync.dma_start(out=gate_sb[:, : 2 * C], in_=gate[:, : 2 * C])
+        nc.sync.dma_start(out=gate_sb[:, 2 * C :], in_=gate[:, 2 * C :])
 
-        def gather_words(a, h):
-            s = slice(h * HALF, (h + 1) * HALF)
-            nc.vector.tensor_copy(g_codes[a][:, s], codes[a][:].indirect(offs_sb[:, h * 48 : h * 48 + 48]))
+        def gather_words(h):
+            t = held.tile([P, HALF], U32, name=f"last{h}", tag="words" if h else "last0", align_bytes=64)
+            nc.vector.tensor_copy(t[:], codes[PASSES - 1][:].indirect(offs_sb[:, h * 48 : h * 48 + 48]))
+            last_codes.append(t)
 
         def gather_bytes(h):
-            s = slice(h * HALF, (h + 1) * HALF)
-            nc.vector.tensor_copy(g_planes[:, s], planes[:].indirect(offs_sb[:, h * 48 : h * 48 + 48]))
+            t = held.tile([P, HALF], U8, name=f"planes{h}", tag="bytes" if h else "planes0", align_bytes=64)
+            nc.vector.tensor_copy(t[:], planes[:].indirect(offs_sb[:, h * 48 : h * 48 + 48]))
+            g_planes.append(t)
 
         for a in range(PASSES):
-            for c0, cw, ns, ends in CHUNKS[a]:
-                grp = xgrp.tile([P, cw, PACK], BF16, name=f"grp{cw}", bufs=1 if cw > 512 else 3, align_bytes=64)
+            for c0, cw, ns in CHUNKS[a]:
+                grp = xgrp.tile([P, cw, PACK], BF16, name=f"grp{cw}", align_bytes=64)
                 to = grp[:].rearrange("p (c i) t -> p c t i", i=4)
-                lo = 0
-                for hi in ends:
-                    fr = raw[a, c0 + lo][:].rearrange("p t (c i) -> p c t i", i=4)
-                    mid = min(max(ns, lo), hi)
-                    if mid > lo:
-                        nc.scalar.activation(to[:, lo // 4 : mid // 4], fr[:, : (mid - lo) // 4], ACT.Copy)
-                    if hi > mid:
-                        nc.vector.tensor_copy(to[:, mid // 4 : hi // 4], fr[:, (mid - lo) // 4 :])
-                    lo = hi
-                flat = grp[:].rearrange("p w t -> p (w t)")
+                fr = raw[a, c0][:].rearrange("p t (c i) -> p c t i", i=4)
+                mid = ns // 4
+                nc.scalar.activation(to[:, :mid], fr[:, :mid], ACT.Copy)
+                if ns < cw:
+                    nc.vector.tensor_copy(to[:, mid:], fr[:, mid:])
                 nc.vector.quantize_mx(
                     out=codes[a][:, c0 : c0 + cw].bitcast(FP8X4),
                     scales=planes[QUAD * a : P, c0 : c0 + cw],
-                    in_=flat,
+                    in_=grp[:].rearrange("p w t -> p (w t)"),
                 )
             if a < PASSES - 1:
                 nc.vector.tensor_copy(g_codes[a][:], codes[a][:].indirect(offs_sb[:]))
 
         flat_codes = w_codes[:].rearrange("p e a n -> p (e a n)")
         flat_planes = w_planes[:].rearrange("p e a n -> p (e a n)")
-        flat_grp = w_grp[:].rearrange("p e a n t -> p (e a n t)")
+        w_grp = []
+        for g in range(E // 2):
+            big = held.tile([P, 4, N, PACK], BF16, name=f"w_big{g}", tag=f"big{g}" if g else "words", align_bytes=64)
+            small = held.tile([P, 2, N, PACK], BF16, name=f"w_small{g}", tag=f"small{g}" if g else "bytes", align_bytes=64)
+            w_grp.append((big, small))
 
         def w_copy(e):
             for a in range(PASSES):
-                to = w_grp[:, e, a].rearrange("p (c i) t -> p c t i", i=4)
+                unit = e % 2 * PASSES + a
+                tile = w_grp[e // 2][unit // 4]
+                to = tile[:, unit % 4].rearrange("p (c i) t -> p c t i", i=4)
                 fr = w_raw[e][:, a].rearrange("p (t c i) -> p c t i", t=PACK, i=4)
-                if e in GPSIMD_EXPERTS:
+                if a == GPSIMD_PASS:
                     nc.gpsimd.tensor_scalar(to, fr, 1.0, 0.0, MULT, ADD)
                 else:
                     nc.scalar.activation(to, fr, ACT.Copy)
 
-        def w_quant(e):
-            base = e * PASSES * N
-            for lo, hi in ((0, 512), (512, 768)):
+        def w_quant(g):
+            lo = g * 2 * PASSES * N
+            for tile, width in zip(w_grp[g], (4 * N, 2 * N)):
                 nc.vector.quantize_mx(
-                    out=flat_codes[:, base + lo : base + hi].bitcast(FP8X4),
-                    scales=flat_planes[:, base + lo : base + hi],
-                    in_=flat_grp[:, PACK * (base + lo) : PACK * (base + hi)],
+                    out=flat_codes[:, lo : lo + width].bitcast(FP8X4),
+                    scales=flat_planes[:, lo : lo + width],
+                    in_=tile[:].rearrange("p u n t -> p (u n t)"),
                 )
+                lo += width
 
         relu = [held.tile([P, 2 * C], F32, name=f"relu{g}") for g in range(E // 2)]
 
         def multiply(e):
             acc = psum.tile([P, C], F32, name=f"acc{e}")
             cols = slice(e * C, (e + 1) * C)
+            in_half = slice(e % 3 * C, (e % 3 + 1) * C)
             for a in range(PASSES):
                 nc.tensor.matmul_mx(
                     out=acc[:],
                     lhsT=w_codes[:, e, a, :].bitcast(FP8X4),
                     lhsT_scale=w_planes[:, e, a, :],
-                    rhs=g_codes[a][:, cols].bitcast(FP8X4),
-                    rhs_scale=g_planes[QUAD * a : P, cols],
+                    rhs=(g_codes[a][:, cols] if a < PASSES - 1 else last_codes[e // 3][:, in_half]).bitcast(FP8X4),
+                    rhs_scale=g_planes[e // 3][QUAD * a : P, in_half],
                     start=(a == 0),
                     stop=(a == PASSES - 1),
                 )
@@ -165,21 +168,23 @@ def tile_moe_two_lin_relu2_kernel(tc, xT, w, b, gate, offs, dst, out):
                 out_sb[:].indirect(dst_sb[:, g * 32 : (g + 1) * 32]), relu[g][:], gate_sb[:, cols], MULT
             )
 
-        for e in range(E):
-            w_copy(e)
-            if e == 1:
-                gather_words(2, 0)
-                gather_bytes(0)
-                w_quant(0)
-                gather_words(2, 1)
-                gather_bytes(1)
-            if e == 3:
-                w_quant(2)
-                multiply(0)
-                multiply(1)
-                square(0)
-                scatter(0)
-        w_quant(4)
+        w_copy(0)
+        w_copy(1)
+        gather_words(0)
+        gather_bytes(0)
+        w_quant(0)
+        w_copy(2)
+        w_copy(3)
+        w_copy(4)
+        gather_words(1)
+        gather_bytes(1)
+        w_quant(1)
+        multiply(0)
+        multiply(1)
+        square(0)
+        scatter(0)
+        w_copy(5)
+        w_quant(2)
         multiply(2)
         multiply(3)
         square(1)

@@ -22,10 +22,10 @@ QUAD = 4
 HALF = T // 2
 WINDOW = 2048
 
-CHUNKS = (
-    ((0, 512, 288), (512, 512, 512), (1024, 512, 512)),
-    ((0, 512, 512), (512, 512, 512), (1024, 512, 384)),
-    ((0, 512, 512), (512, 512, 448), (1024, 256, 160), (1280, 256, 96)),
+LOADS = (
+    (((512, 256), (512, 128)), ((512, 256),)),
+    (((512, 352), (512, 304)), ((512, 208),)),
+    (((512, 512),), ((512, 416),), ((256, 256),), ((256, 96),)),
 )
 GPSIMD_PASS = 2
 ADD = mybir.AluOpType.add
@@ -63,13 +63,19 @@ def tile_moe_two_lin_relu2_kernel(tc, xT, w, b, gate, offs, dst, out):
         nc.gpsimd.memset(warm[:], 0.0)
         nc.scalar.activation(warm[:], warm[:], ACT.Relu)
 
-        raw = {}
+        pieces = [[] for a in range(PASSES)]
         for a in range(PASSES):
             rows = xT[a * 512 : (a + 1) * 512, :].rearrange("(p j) t -> p j t", j=PACK)
-            for c0, cw, ns in CHUNKS[a]:
-                t = xraw.tile([P, PACK, cw], F32, name=f"x{a}_{c0}")
-                nc.sync.dma_start(out=t[:], in_=rows[:, :, c0 : c0 + cw])
-                raw[a, c0] = t
+            first = 0
+            for i, tiles in enumerate(LOADS[a]):
+                width = sum(cw for cw, ns in tiles)
+                raw = xraw.tile([P, PACK, width], F32, name=f"x{a}_{i}")
+                nc.sync.dma_start(out=raw[:], in_=rows[:, :, first : first + width])
+                lo = 0
+                for cw, ns in tiles:
+                    pieces[a].append((raw[:, :, lo : lo + cw], first + lo, cw, ns))
+                    lo += cw
+                first += width
             if a == 0:
                 nc.sync.dma_start(offs_sb[:], offs)
         w_raw = []
@@ -95,10 +101,10 @@ def tile_moe_two_lin_relu2_kernel(tc, xT, w, b, gate, offs, dst, out):
             g_planes.append(t)
 
         for a in range(PASSES):
-            for c0, cw, ns in CHUNKS[a]:
+            for src, c0, cw, ns in pieces[a]:
                 grp = xgrp.tile([P, cw, PACK], BF16, name=f"grp{cw}", align_bytes=64)
                 to = grp[:].rearrange("p (c i) t -> p c t i", i=4)
-                fr = raw[a, c0][:].rearrange("p t (c i) -> p c t i", i=4)
+                fr = src.rearrange("p t (c i) -> p c t i", i=4)
                 mid = ns // 4
                 nc.scalar.activation(to[:, :mid], fr[:, :mid], ACT.Copy)
                 if ns < cw:
@@ -125,10 +131,12 @@ def tile_moe_two_lin_relu2_kernel(tc, xT, w, b, gate, offs, dst, out):
                 tile = w_grp[e // 2][unit // 4]
                 to = tile[:, unit % 4].rearrange("p (c i) t -> p c t i", i=4)
                 fr = w_raw[e][:, a].rearrange("p (t c i) -> p c t i", t=PACK, i=4)
-                if a == GPSIMD_PASS:
+                if a < PASSES - 1:
+                    nc.scalar.activation(to, fr, ACT.Copy)
+                elif e < E - 1:
                     nc.gpsimd.tensor_scalar(to, fr, 1.0, 0.0, MULT, ADD)
                 else:
-                    nc.scalar.activation(to, fr, ACT.Copy)
+                    nc.vector.tensor_copy(to, fr)
 
         def w_quant(g):
             lo = g * 2 * PASSES * N

from contextlib import ExitStack

import concourse.mybir as mybir

K, T, E, C, N = 1536, 1536, 6, 256, 128
FLOPS = 2 * E * C * K * N

F32 = mybir.dt.float32
BF16 = mybir.dt.bfloat16
U32 = mybir.dt.uint32
I32 = mybir.dt.int32
U16 = mybir.dt.uint16
U8 = mybir.dt.uint8
FP8X4 = mybir.dt.float8_e4m3fn_x4
ACT = mybir.ActivationFunctionType
MULT = mybir.AluOpType.mult

P = 128
PACK = 4
PASSES = K // (P * PACK)
QUAD = 4
HALF = T // 2
WINDOW = 2048

LOADS = (
    (((512, 256), (512, 128)), ((512, 256),)),
    (((512, 352), (512, 304)), ((512, 208),)),
    (((512, 512),), ((512, 416),), ((256, 256),), ((256, 96),)),
)
GPSIMD_PASS = 2
ADD = mybir.AluOpType.add


def tile_moe_two_lin_relu2_kernel(tc, xT, w, b, gate, offs, dst, out):
    nc = tc.nc
    with ExitStack() as ctx:
        held = ctx.enter_context(tc.tile_pool(name="held", bufs=1))
        xraw = ctx.enter_context(tc.tile_pool(name="xraw", bufs=1))
        xgrp = ctx.enter_context(tc.tile_pool(name="xgrp", bufs=3))
        wraw = ctx.enter_context(tc.tile_pool(name="wraw", bufs=1))
        psum = ctx.enter_context(tc.psum_pool(name="psum", bufs=1))

        offs_sb = held.tile([P, T // 16], U16, name="offs_sb")
        dst_sb = held.tile([P, T // 16], U16, name="dst_sb")
        bias = held.tile([P, E], F32, name="bias")
        gate_sb = held.tile([P, T], F32, name="gate_sb", align_bytes=64)
        out_sb = held.tile([P, T], F32, name="out_sb", align_bytes=64)
        planes = held.tile([P, T], U8, name="planes", align_bytes=64)
        codes = [
            held.tile([P, T if a == PASSES - 1 else WINDOW], U32, name=f"codes{a}", align_bytes=64)
            for a in range(PASSES)
        ]
        g_codes = [held.tile([P, T], U32, name=f"g_codes{a}", align_bytes=64) for a in range(PASSES - 1)]
        last_codes = []
        g_planes = []
        w_codes = held.tile([P, E, PASSES, N], U32, name="w_codes", align_bytes=64)
        w_planes = held.tile([P, E, PASSES, N], U8, name="w_planes", align_bytes=64)
        warm = held.tile([P, 1], F32, name="warm")

        nc.gpsimd.memset(planes[:].bitcast(I32), 0)
        for a in range(PASSES - 1):
            nc.gpsimd.memset(codes[a][:, T:].bitcast(I32), 0)
        nc.gpsimd.memset(warm[:], 0.0)
        nc.scalar.activation(warm[:], warm[:], ACT.Relu)

        pieces = [[] for a in range(PASSES)]
        for a in range(PASSES):
            rows = xT[a * 512 : (a + 1) * 512, :].rearrange("(p j) t -> p j t", j=PACK)
            first = 0
            for i, tiles in enumerate(LOADS[a]):
                width = sum(cw for cw, ns in tiles)
                raw = xraw.tile([P, PACK, width], F32, name=f"x{a}_{i}")
                nc.sync.dma_start(out=raw[:], in_=rows[:, :, first : first + width])
                lo = 0
                for cw, ns in tiles:
                    pieces[a].append((raw[:, :, lo : lo + cw], first + lo, cw, ns))
                    lo += cw
                first += width
            if a == 0:
                nc.sync.dma_start(offs_sb[:], offs)
        w_raw = []
        for e in range(E):
            t = wraw.tile([P, PASSES, PACK * N], F32, name=f"w{e}")
            nc.sync.dma_start(out=t[:], in_=w[e].rearrange("(a p j) n -> p a (j n)", p=P, j=PACK))
            w_raw.append(t)
            if e == 0:
                nc.sync.dma_start(dst_sb[:], dst)
            if e == 3:
                nc.sync.dma_start(out=bias[:], in_=b)
                nc.sync.dma_start(out=gate_sb[:, : 2 * C], in_=gate[:, : 2 * C])
        nc.sync.dma_start(out=gate_sb[:, 2 * C :], in_=gate[:, 2 * C :])

        def gather_words(h):
            t = held.tile([P, HALF], U32, name=f"last{h}", tag="words" if h else "last0", align_bytes=64)
            nc.vector.tensor_copy(t[:], codes[PASSES - 1][:].indirect(offs_sb[:, h * 48 : h * 48 + 48]))
            last_codes.append(t)

        def gather_bytes(h):
            t = held.tile([P, HALF], U8, name=f"planes{h}", tag="bytes" if h else "planes0", align_bytes=64)
            nc.vector.tensor_copy(t[:], planes[:].indirect(offs_sb[:, h * 48 : h * 48 + 48]))
            g_planes.append(t)

        for a in range(PASSES):
            for src, c0, cw, ns in pieces[a]:
                grp = xgrp.tile([P, cw, PACK], BF16, name=f"grp{cw}", align_bytes=64)
                to = grp[:].rearrange("p (c i) t -> p c t i", i=4)
                fr = src.rearrange("p t (c i) -> p c t i", i=4)
                mid = ns // 4
                nc.scalar.activation(to[:, :mid], fr[:, :mid], ACT.Copy)
                if ns < cw:
                    nc.vector.tensor_copy(to[:, mid:], fr[:, mid:])
                nc.vector.quantize_mx(
                    out=codes[a][:, c0 : c0 + cw].bitcast(FP8X4),
                    scales=planes[QUAD * a : P, c0 : c0 + cw],
                    in_=grp[:].rearrange("p w t -> p (w t)"),
                )
            if a < PASSES - 1:
                nc.vector.tensor_copy(g_codes[a][:], codes[a][:].indirect(offs_sb[:]))

        flat_codes = w_codes[:].rearrange("p e a n -> p (e a n)")
        flat_planes = w_planes[:].rearrange("p e a n -> p (e a n)")
        w_grp = []
        for g in range(E // 2):
            big = held.tile([P, 4, N, PACK], BF16, name=f"w_big{g}", tag=f"big{g}" if g else "words", align_bytes=64)
            small = held.tile([P, 2, N, PACK], BF16, name=f"w_small{g}", tag=f"small{g}" if g else "bytes", align_bytes=64)
            w_grp.append((big, small))

        def w_copy(e):
            for a in range(PASSES):
                unit = e % 2 * PASSES + a
                tile = w_grp[e // 2][unit // 4]
                to = tile[:, unit % 4].rearrange("p (c i) t -> p c t i", i=4)
                fr = w_raw[e][:, a].rearrange("p (t c i) -> p c t i", t=PACK, i=4)
                if a < PASSES - 1:
                    nc.scalar.activation(to, fr, ACT.Copy)
                elif e < E - 1:
                    nc.gpsimd.tensor_scalar(to, fr, 1.0, 0.0, MULT, ADD)
                else:
                    nc.vector.tensor_copy(to, fr)

        def w_quant(g):
            lo = g * 2 * PASSES * N
            for tile, width in zip(w_grp[g], (4 * N, 2 * N)):
                nc.vector.quantize_mx(
                    out=flat_codes[:, lo : lo + width].bitcast(FP8X4),
                    scales=flat_planes[:, lo : lo + width],
                    in_=tile[:].rearrange("p u n t -> p (u n t)"),
                )
                lo += width

        relu = [held.tile([P, 2 * C], F32, name=f"relu{g}") for g in range(E // 2)]

        def multiply(e):
            acc = psum.tile([P, C], F32, name=f"acc{e}")
            cols = slice(e * C, (e + 1) * C)
            in_half = slice(e % 3 * C, (e % 3 + 1) * C)
            for a in range(PASSES):
                nc.tensor.matmul_mx(
                    out=acc[:],
                    lhsT=w_codes[:, e, a, :].bitcast(FP8X4),
                    lhsT_scale=w_planes[:, e, a, :],
                    rhs=(g_codes[a][:, cols] if a < PASSES - 1 else last_codes[e // 3][:, in_half]).bitcast(FP8X4),
                    rhs_scale=g_planes[e // 3][QUAD * a : P, in_half],
                    start=(a == 0),
                    stop=(a == PASSES - 1),
                )
            half = e % 2 * C
            nc.scalar.activation(relu[e // 2][:, half : half + C], acc[:], ACT.Relu, bias=bias[:, e : e + 1])

        def square(g):
            nc.scalar.activation(relu[g][:], relu[g][:], ACT.Square)

        def scatter(g):
            cols = slice(g * 2 * C, (g + 1) * 2 * C)
            nc.vector.tensor_tensor(
                out_sb[:].indirect(dst_sb[:, g * 32 : (g + 1) * 32]), relu[g][:], gate_sb[:, cols], MULT
            )

        w_copy(0)
        w_copy(1)
        gather_words(0)
        gather_bytes(0)
        w_quant(0)
        w_copy(2)
        w_copy(3)
        w_copy(4)
        gather_words(1)
        gather_bytes(1)
        w_quant(1)
        multiply(0)
        multiply(1)
        square(0)
        scatter(0)
        w_copy(5)
        w_quant(2)
        multiply(2)
        multiply(3)
        square(1)
        scatter(1)
        multiply(4)
        multiply(5)
        square(2)
        scatter(2)
        nc.sync.dma_start(out=out, in_=out_sb[:])
